import numpy as np, ml_dtypes
CORES = [16,18,20,22]
N = 4
BF = ml_dtypes.bfloat16
def gentries(a):
    return np.ascontiguousarray(a.reshape(8, 16, -1).transpose(0, 2, 1)).reshape(8, -1)
def gtable(e):
    e = np.asarray(e); return np.ascontiguousarray(e.reshape(8, -1, 16).transpose(0, 2, 1)).reshape(128, -1).astype(np.int32)
V, RO, VO, GS = 2048, 3, 9, 1
def mix(rng, p):
    return [p[i] for i in rng.permutation(len(p))]
def invol(rng, n):
    o = rng.permutation(V); t = np.arange(V); t[o[n::2]] = o[n + 1::2]; t[o[n + 1::2]] = o[n::2]
    return t
def sew(parts, line):
    t = np.arange(V); s = np.arange(V); at = 0
    for n, kind in parts:
        w = line[at:at + n]; at += n
        if n == 1: continue
        two = (t, s) if kind == 1 else (s, t)
        for q in (0, 1):
            e = w[q:]; m = len(e) // 2 * 2; a = e[0:m:2]; b = e[1:m:2]
            two[q][a] = b; two[q][b] = a
        if kind == 2: t[w[0]] = w[n - 1]; t[w[n - 1]] = w[0]
    return t, s
def tie(rng, s, goal, straight):
    v = np.arange(V); u = np.empty(V, np.int64); a = v[s > v]; z = v[goal > v]
    u[rng.permutation(v[s == v])] = v[goal == v]
    if straight: z = goal[z]
    else: a = rng.permutation(a); z = np.where(rng.random(len(z)) < 0.5, z, goal[z])
    u[a] = z; u[s[a]] = goal[z]
    return u
def grow(rng, parts, lines, straight=False):
    b = [sew(parts[r], lines[r]) for r in range(N)]; t = np.stack([y[0] for y in b])
    return t, np.stack([tie(rng, b[r][1], t[(r + 1) % N], straight) for r in range(N)])
def cut(rng, n, top, ring):
    out = []; left = V
    for i in range(n // 2):
        if rng.random() < 0.5: z = 2 * rng.integers(0, top // 2, 2) + 1; y = rng.integers(0, 2, 2)
        else: z = 2 * rng.integers(1, top // 2 + 1, 2); y = (0, 1)
        out += [(int(z[0]), int(y[0])), (int(z[1]), int(y[1]))]; left -= int(z[0] + z[1])
    while left > 0:
        m = min(left, 2 * int(rng.integers(1, ring + 1))); out.append((m, 2)); left -= m
    return mix(rng, out)
CUTS = ((64, 16, 10), (128, 8, 6), (16, 64, 40), (4, 256, 150))
def base(rng):
    t = np.empty((N, 8, V), np.int64); u = np.empty((N, 8, V), np.int64); o = rng.permutation(8)
    for q in range(8):
        g = o[q]
        if q < 4:
            for r in range(N):
                n = int(rng.choice(np.array([0, 2]))) if q == 0 else 2 * int(rng.choice(np.array([0, 1, V // 64, V // 32, V // 16, V // 8, V // 4])))
                t[r, g] = invol(rng, n); u[r, g] = rng.permutation(V)
        else:
            n, top, ring = CUTS[q - 4]
            t[:, g], u[:, g] = grow(rng, [cut(rng, n, top, ring) for r in range(N)], [rng.permutation(V) for r in range(N)])
    return t, u
def hang(rng):
    n = np.array([VO, VO - 1, 16, 0, VO, VO - 1, 15, VO + 1])[(np.arange(8)[None, :] + np.arange(N)[:, None] + rng.integers(0, 8)) % 8][:, :, None, None]
    ok = np.argsort(rng.random((N, 8, 16, 1)), axis=2) < n
    th = rng.choice(np.array([0, 1, 7, 100, 253, 254]), (N, 8, 16, 1)); gap = th + 1 - ok.astype(np.int64)
    low = np.floor(rng.random((N, 8, 16, 1)) * (256 - gap)).astype(np.int64); share = rng.choice(np.array([0.004, 0.03, 0.2, 0.5]), (N, 8, 1, 1))
    hi = (rng.random((N, 8, 1, V)) < share) & (rng.random((N, 8, 16, V)) < 0.75)
    return low + gap * hi, th
def pack(t, u, x, th):
    return {"t0": np.stack([gtable(a) for a in t]), "u0": np.stack([gtable(a) for a in u]),
            "x": np.ascontiguousarray(x.reshape(N, 128, V)).astype(np.float32).astype(BF), "th": np.ascontiguousarray(th.reshape(N, 128, 1)).astype(np.int32)}
def setup_inputs(rng):
    t, u = base(rng)
    th = rng.integers(8, 120, (N, 8, 16, 1)); low = np.floor(rng.random((N, 8, 16, 1)) * (256 - th)).astype(np.int64)
    x = low + np.floor(rng.random((N, 8, 16, V)) * (th + 1)).astype(np.int64)
    share = rng.choice(np.array([0.004, 0.015, 0.04, 0.12]), (N, 8, 1, 1))
    m = (rng.random((N, 8, 1, V)) < share) & (rng.random((N, 8, 16, V)) < rng.random((N, 8, 1, V)))
    return pack(t, u, np.where(m, rng.integers(0, 256, m.shape), x), th)
def setup_inputs_spread(rng):
    t, u = base(rng)
    th = np.floor(np.exp2(8 * rng.random((N, 8, 16, 1)))).astype(np.int64) - (rng.random((N, 8, 16, 1)) < 0.25)
    e = rng.choice(np.array([1.0, 3.0, 8.0]), (N, 8, 1, 1))
    x = np.floor(np.exp2(8 * rng.random((N, 8, 1, V)) ** e) * rng.random((N, 8, 16, V))).astype(np.int64)
    return pack(t, u, x, th)
def setup_inputs_ends(rng):
    zig = np.empty(V, np.int64); zig[0::2] = np.arange(V // 2); zig[1::2] = V - 1 - np.arange(V // 2)
    t = np.empty((N, 8, V), np.int64); u = np.empty((N, 8, V), np.int64)
    for g in range(8):
        if g < 3: lines = [np.roll(zig, 2 * int(rng.integers(0, V // 2))) for r in range(N)]
        elif g < 6: lines = [zig.reshape(-1, 16)[rng.permutation(V // 16)].reshape(-1) for r in range(N)]
        else: lines = [np.arange(V)[::(1, -1)[(r + g) % 2]] for r in range(N)]
        if g == 0: parts = [[(V, r % 2)] for r in range(N)]
        elif g == 1: parts = [[(V - 1, int(rng.integers(0, 2))), (1, 0)] for r in range(N)]
        elif g == 2: parts = [[(V, 2)] for r in range(N)]
        else: parts = [cut(rng, *CUTS[(2, 0, 3, 1, 0)[g - 3]]) for r in range(N)]
        t[:, g], u[:, g] = grow(rng, parts, lines, g % 2 == 1)
    n = np.stack([rng.permutation(np.array([VO, VO - 1, VO - 2, VO - 1, VO - 1, 0, 16, 15])) for r in range(N)])[:, :, None, None]
    all_ = np.argsort(rng.random((N, 8, 16, 1)), axis=2) < n; th = 255 * all_.astype(np.int64)
    e = rng.integers(0, 2, (N, 8, 16, 1)); share = rng.choice(np.array([0.003, 0.02, 0.06]), (N, 8, 1, 1))
    m = (rng.random((N, 8, 1, V)) < share) & (rng.random((N, 8, 16, V)) < rng.random((N, 8, 1, V)))
    m[:, 1::2, :, V - 1] = True; m[:, 0::2, :, 0] = True
    m = np.where(all_, rng.random(m.shape) < 0.5, m)
    return pack(t, u, 255 * (e ^ m.astype(np.int64)), th)
def setup_inputs_corners(rng):
    t = np.empty((N, 8, V), np.int64); u = np.empty((N, 8, V), np.int64); o = rng.permutation(8)
    for q in range(8):
        g = o[q]; lines = [rng.permutation(V) for r in range(N)]
        if q == 0: parts = [[(V, r % 2)] for r in range(N)]
        elif q == 1:
            parts = [[(V - 1, int(rng.integers(0, 2))), (1, 0)] for r in range(N)]; lines = [np.append(rng.permutation(V - 1), V - 1) for r in range(N)]
        elif q == 2: parts = [[(V, 2)] for r in range(N)]
        elif q == 3: parts = [[(V - 2, 2), (2, 2)] for r in range(N)]
        elif q == 4:
            m = V // 6 // 2 * 2; left = V - 4 * (V // 8) - 3 * m
            p = [(2, 0)] * (V // 8) + [(2, 1)] * (V // 8) + [(3, 0)] * (m // 2) + [(3, 1)] * (m // 2) + ([(left, 2)] if left else [])
            parts = [mix(rng, p) for r in range(N)]
        elif q == 5: parts = [mix(rng, [(4, 2), (8, 2), (4, 2)] * (V // 16)) for r in range(N)]
        elif q == 6:
            z = int(rng.integers(0, N))
            for r in range(N): t[r, g] = invol(rng, V if r == z else 2 * int(rng.choice(np.array([0, 1, V // 16, V // 4])))); u[r, g] = rng.permutation(V)
            continue
        else: parts = [cut(rng, *CUTS[0]) for r in range(N)]
        t[:, g], u[:, g] = grow(rng, parts, lines)
    x, th = hang(rng)
    return pack(t, u, x, th)
def setup_inputs_lone(rng):
    t = np.empty((N, 8, V), np.int64); u = np.empty((N, 8, V), np.int64); o = rng.permutation(8)
    pairs = [(2, 0)] * (V // 8) + [(2, 1)] * (V // 8) + [(4, 2)] * (V // 8)
    few = [(3, 0)] * (V // 128) + [(3, 1)] * (V // 128) + [(2, 0)] * (V // 64) + [(2, 1)] * (V // 64) + [(4, 2)] * (V // 128)
    m = 10 * (V // 128) + 4 * (V // 64); still = [(2, 2)] * (V // 8) + [(1, 0)] * (V - m - 2 * (V // 8))
    for q in range(8):
        g = o[q]; lines = [rng.permutation(V) for r in range(N)]
        if q < 2: parts = [[(V, r % 2)] for r in range(N)]
        elif q == 2: parts = [[(V - 16, r % 2), (16, 2)] for r in range(N)]
        elif q < 5:
            parts = [mix(rng, pairs) for r in range(N)]
            if q == 4: lines = [np.arange(V)[::(1, -1)[r % 2]] for r in range(N)]
        elif q == 5:
            parts = [still + mix(rng, few) for r in range(N)]; lines = [np.concatenate([rng.permutation(V - m), V - m + rng.permutation(m)]) for r in range(N)]
        elif q == 6:
            parts = [[(1, 0)] * (V - 2) + [(2, r % 2)] for r in range(N)]; lines = [np.append(rng.permutation(V - 2), [V - 2, V - 1]) for r in range(N)]
        else: parts = [mix(rng, still + few) for r in range(N)]
        t[:, g], u[:, g] = grow(rng, parts, lines)
    pos = np.argsort(rng.random((N, 8, 16, 1)), axis=2); th = rng.choice(np.array([0, 1, 7, 100, 253, 254]), (N, 8, 16, 1))
    low = np.floor(rng.random((N, 8, 16, 1)) * (255 - th)).astype(np.int64); step = th + (pos >= VO - 1).astype(np.int64)
    x = low + step * rng.integers(0, 2, (N, 8, 1, V))
    for r in range(N):
        for q in range(8):
            g = int(o[q]); s = np.argsort(u[r, g])[t[(r + 1) % N, g][u[r, g]]]; row, first = orbits(t[r, g][s]); size = np.diff(np.append(first, V))
            i = int(np.argmax(pos[r, g, :, 0] == VO - 1)); a = int(low[r, g, i, 0]); b = int(th[r, g, i, 0])
            if q < 3:
                k = int(np.argmax(size)); n = int(size[k]) // 2; j = n - 1 if q == 1 else int(rng.integers(V // 3, n))
                x[r, g, i] = a; x[r, g, i, int(row[int(first[k]) + j + n * int(rng.integers(0, 2))])] = a + b + (r + q) % 2
            else:
                k = int(np.flatnonzero(size % 2 == 0)[-1]); v = int(row[first[k]]); w = int(row[first[k] + 1])
                x[r, g, :, v] = low[r, g, :, 0]; x[r, g, :, w] = low[r, g, :, 0] + step[r, g, :, 0]; x[r, g, i, w] = a + b
    return pack(t, u, x, th)
def setup_inputs_votes(rng):
    t, u = base(rng); x, th = hang(rng)
    return pack(t, u, x, th)
def check_inputs(d):
    bad = []
    for k, lo, hi in (("t0", 0, V - 1), ("u0", 0, V - 1), ("x", 0, 255), ("th", 0, 255)):
        a = np.asarray(d[k]).astype(np.float64)
        if not (np.min(a) >= lo and np.max(a) <= hi): bad.append("range of " + k)
        elif np.any(a != np.floor(a)): bad.append("whole numbers in " + k)
    if not bad:
        t = np.stack([gentries(a) for a in np.asarray(d["t0"])]).astype(np.int64); u = np.stack([gentries(a) for a in np.asarray(d["u0"])]).astype(np.int64)
        if np.any(np.take_along_axis(t, t, 2) != np.arange(V)): bad.append("t0 holds involutions")
        if np.any(np.sort(u, axis=2) != np.arange(V)): bad.append("u0 holds permutations")
    return bad
def orbits(c):
    c = c.tolist(); seen = bytearray(V); row = []; first = []
    for v in range(V):
        if not seen[v]:
            first.append(len(row))
            while not seen[v]:
                seen[v] = 1; row.append(v); v = c[v]
    return np.array(row), np.array(first)
def reference(t0, u0, x, th):
    t = np.stack([gentries(a) for a in t0]).astype(np.int64); u = np.stack([gentries(a) for a in u0]).astype(np.int64)
    xs = x.astype(np.float32).reshape(N, 8, 16, V); lim = th.astype(np.float32).reshape(N, 8, 16, 1)
    for rnd in range(RO):
        tn = np.empty_like(t); un = np.empty_like(u)
        for r in range(N):
            for g in range(8):
                far = t[(r + 1) % N, g]
                s = np.argsort(u[r, g])[far[u[r, g]]]; c = t[r, g][s]
                row, first = orbits(c); size = np.diff(np.append(first, V))
                start = np.repeat(first, size); o = np.repeat(size, size)
                half = row[start + (np.arange(V) - start + o // 2) % o]
                gap = np.abs(xs[r, g][:, row] - xs[r, g][:, half])
                top = np.maximum.reduceat(gap, first, axis=1)
                votes = np.add.reduce((top <= lim[r, g]).astype(np.int64), axis=0)
                turn = np.repeat((size % 2 == 1) | (votes >= VO), size)
                k = np.empty(V, np.int64); k[row] = np.where(turn, half, row)
                h = u[r, g][k]
                tn[r, g] = np.argsort(h)[far[h]]; un[(r + 1) % N, (g + GS) % 8] = h
        t, u = tn, un
    return {"yt": np.stack([gtable(a) for a in t]).astype(np.float32), "yu": np.stack([gtable(a) for a in u]).astype(np.float32)}

from concourse.mybir import AluOpType as ALU, ActivationFunctionType as ACT

V = 2048
RO = 3
STEPS = 11
GS = 1
F32, BF, F16, I32, U16 = "float32", "bfloat16", "float16", "int32", "uint16"

SCRATCH = {}
for _n in ("YA", "YB", "IN1", "TMP", "WE", "IN2", "S1", "ST"):
    SCRATCH[_n] = ("sbuf", [128, V], F32)
for _n in ("CB", "CB0", "RW", "HB", "XB", "X2", "NEG", "EG", "EGS", "S2"):
    SCRATCH[_n] = ("sbuf", [128, V], BF)
SCRATCH["AW"] = ("sbuf", [128, V + 16], BF)
SCRATCH["LO"] = ("sbuf", [128, V], F16)
SCRATCH["LL"] = ("sbuf", [128, 384], U16)
LISTS = {"LR": 0, "Lend": 128, "Ls": 256}
HI, LOW, KE, KO, PH, PL, SH, SL = 0, 1, 3, 4, 6, 7, 8, 9
for _n in ("t0i", "u0i"):
    SCRATCH[_n] = ("sbuf", [128, 128], I32)
for _n in ("Lc", "La", "Lb", "Ll", "Lslot", "Lsh", "Lhalf",
           "uL0", "uL1", "uL2", "fL0", "fL1", "fL2", "fS0", "fS1", "fS2", "hS0", "hS1"):
    SCRATCH[_n] = ("sbuf", [128, 128], U16)
for _n in ("hF", "uF", "tf", "uf", "Kw", "slotf", "of", "a1", "af", "mo", "sf", "r1", "r2",
           "Tn", "Ts", "xr", "p2", "IC", "IX", "IG", "BLF", "I32", "N32", "N2", "BK"):
    SCRATCH[_n] = ("sbuf", [128, 128], F32)
for _n in ("thi", "tlo", "uhi", "ulo", "odd", "sg", "I2k", "Ix", "Ixn", "Im64", "I4k", "N4k", "Nb", "SelP"):
    SCRATCH[_n] = ("sbuf", [128, 128], BF)
for _n in ("pu", "BL"):
    SCRATCH[_n] = ("sbuf", [128, 128], F16)
SCRATCH["B2"] = ("sbuf", [128, 256], F16)
SCRATCH["B4"] = ("sbuf", [128, 256], F32)
for _n, _d in (("Z01", BF), ("ZP", BF), ("ZS", BF), ("Z1", BF), ("ZK", F32), ("ZX", F16), ("ZO", F16), ("ZE", F16), ("ZJ", F16), ("SelS", BF)):
    SCRATCH[_n] = ("sbuf", [128, 144], _d)
SCRATCH["ZI"] = ("sbuf", [128, 512], F32)
for _n in ("MU", "M16", "XA"):
    SCRATCH[_n] = ("sbuf", [128, 512], BF)
for _n in ("RM", "BLK", "AB", "RB", "SB", "col", "cw", "d0", "d1"):
    SCRATCH[_n] = ("sbuf", [128, 16], F32)
SCRATCH["ci"] = ("sbuf", [128, 16], I32)
SCRATCH["thI"] = ("sbuf", [128, 4], I32)
for _n in range(8):
    SCRATCH["P%d" % _n] = ("psum", [128, 512], F32)

SEMAPHORES = ["cv", "cs", "cp", "cg", "ldt", "ldu", "ldx", "ldh", "sent", "out",
              "af0", "af1", "af2", "au1", "au2", "au3"]


def rank_program(g, core, T, topo):
    rank = T.rank_of(core)
    if rank is None:
        return
    n_ranks = len(T.cores)
    nxt = T.cores[(rank + 1) % n_ranks]
    prv = T.cores[(rank - 1) % n_ranks]
    Q = {"v": g.vector, "s": g.scalar, "p": g.tensor, "g": g, "y": g.sync}
    SEM = {"v": "cv", "s": "cs", "p": "cp", "g": "cg"}
    cnt = {"v": 0, "s": 0, "p": 0, "g": 0}
    seen = {k: {} for k in Q}
    log = {}
    sent = [0]

    def wait(q, sem, val):
        if seen[q].get(sem, 0) < val:
            Q[q].wait_ge(T.sem[sem], val)
            seen[q][sem] = val

    def order(q, reads, writes):
        need = {}
        for rs, wr in ((reads, False), (writes, True)):
            for (b, c0, c1) in rs:
                bank = SCRATCH[b][0] == "psum"
                for (d0, d1, e, sem, val, w) in log.get(b, ()):
                    if e == q and q == "p":
                        continue
                    hit = (wr or w) and d0 < c1 and c0 < d1
                    if bank and e != q:
                        hit = True
                    if hit:
                        need[sem] = max(need.get(sem, 0), val)
        for sem in need:
            wait(q, sem, need[sem])

    def note(q, sem, val, reads, writes):
        for (b, c0, c1) in writes:
            log[b] = [r for r in log.get(b, ()) if not (c0 <= r[0] and r[1] <= c1)] + [(c0, c1, q, sem, val, True)]
        for (b, c0, c1) in reads:
            log[b] = [r for r in log.get(b, ()) if not (r[2] == q and not r[5] and c0 <= r[0] and r[1] <= c1)] + [(c0, c1, q, sem, val, False)]

    def op(q, fn, reads, writes):
        order(q, reads, writes)
        ins = fn()
        cnt[q] += 1
        ins.then_inc(T.sem[SEM[q]], 1)
        note(q, SEM[q], cnt[q], reads, writes)

    def R(b, c0=0, c1=None):
        return (b, c0, SCRATCH[b][1][1] if c1 is None else c1)

    def A(r):
        return T[r[0]][:, r[1]:r[2]]

    def L(lst, c0, c1):
        if lst in LISTS:
            return ("LL", LISTS[lst] + c0 // 16, LISTS[lst] + c1 // 16)
        return (lst, c0 // 16, c1 // 16)

    def col(b, j):
        return (b, j, j + 1)

    def sc(x):
        return A(x) if isinstance(x, tuple) else x

    def regs(*xs):
        return [x for x in xs if isinstance(x, tuple)]

    def ind(win, lst, c0, c1):
        return T[win][:, 0:V].indirect(A(L(lst, c0, c1)))

    def vcopy(out, in_, oap=None):
        op("v", lambda: g.vector.tensor_copy(A(out) if oap is None else oap, A(in_)), [in_], [out])

    def vts(out, in_, s1, s2, o0, o1=None, oap=None):
        o = A(out) if oap is None else oap
        if o1 is None:
            op("v", lambda: g.vector.tensor_scalar(o, A(in_), sc(s1), None, o0), [in_] + regs(s1), [out])
        else:
            op("v", lambda: g.vector.tensor_scalar(o, A(in_), sc(s1), sc(s2), o0, o1), [in_] + regs(s1, s2), [out])

    def vtt(out, in0, in1, o):
        op("v", lambda: g.vector.tensor_tensor(A(out), A(in0), A(in1), o), [in0, in1], [out])

    def vset(out, val):
        op("v", lambda: g.vector.memset(A(out), val), [], [out])

    def vscan(out, d0, d1, init, o0, o1):
        op("v", lambda: g.vector.tensor_tensor_scan(A(out), A(d0), A(d1), sc(init), o0, o1), [d0, d1] + regs(init), [out])

    def act(out, in_, func=ACT.Identity, bias=0.0, scale=1.0):
        op("s", lambda: g.scalar.activation(A(out), A(in_), func, bias=sc(bias), scale=sc(scale)), [in_] + regs(bias, scale), [out])

    def gcast(out, in_):
        op("g", lambda: g.affine_select(A(out), A(in_), [[0, in_[2] - in_[1]]], ALU.is_ge, 0.0, 0, 0), [in_], [out])

    def giota(out, pattern, cm, base=0):
        if SCRATCH[out[0]][2] == I32:
            op("g", lambda: g.iota(A(out), pattern, base, cm), [], [out])
        else:
            op("g", lambda: g.iota(A(out), pattern, base, cm, allow_small_or_imprecise_dtypes=True), [], [out])

    def vgather(out, win, lst, c0, c1, in1=None, o=None, clamp=False):
        rd = [R(win), L(lst, c0, c1)]
        dst = (out, c0, c1)
        if in1 is not None:
            op("v", lambda: g.vector.tensor_tensor(A(dst), ind(win, lst, c0, c1), A((in1, c0, c1)), o), rd + [(in1, c0, c1)], [dst])
        elif clamp:
            op("v", lambda: g.vector.tensor_scalar(A(dst), ind(win, lst, c0, c1), -1.0, 1.0, ALU.max, ALU.min), rd, [dst])
        else:
            op("v", lambda: g.vector.tensor_copy(A(dst), ind(win, lst, c0, c1)), rd, [dst])

    def sgather(out, win, lst, c0, c1, clamp=False):
        dst = (out, c0, c1)
        op("s", lambda: g.scalar.activation(A(dst), ind(win, lst, c0, c1), ACT.Sign if clamp else ACT.Identity),
           [R(win), L(lst, c0, c1)], [dst])

    def scatter(win, lst, src, c0, c1):
        op("v", lambda: g.vector.tensor_copy(ind(win, lst, c0, c1), A((src, c0, c1))), [(src, c0, c1), (lst, c0 // 16, c1 // 16)], [R(win)])

    def mm(group, reads, writes, first=True, last=True):
        order("p", reads, writes)
        for k, (o, l, r) in enumerate(group):
            ins = g.tensor.matmul(o, l, r, first and k == 0, last and k == len(group) - 1)
        cnt["p"] += 1
        ins.then_inc(T.sem.cp, 1)
        note("p", "cp", cnt["p"], reads, writes)

    def extract(dst, Z, src, m0, m1, more=(), last=True):
        out = (dst[0], dst[1] + m0, dst[1] + m1)
        grp = [(A(out), T[Z][:, 15 - i:143 - i], T[src][:, 16 * m0 + i:16 * m1:16]) for i in range(16)]
        grp += [(A(out), A(R(l)), T[t][:, m0:m1]) for (l, t) in more]
        mm(grp, [R(Z), (src, 16 * m0, 16 * m1)] + [R(l) for (l, t) in more] + [(t, m0, m1) for (l, t) in more], [out], last=last)

    def combine(dst, terms, first=True, last=True):
        mm([(A(dst), A(R(l)), A(R(t))) for (l, t) in terms], [R(x) for lt in terms for x in lt], [dst], first=first, last=last)

    def prespread(bank):
        combine(R("P%d" % bank), [("SelP", "M16")], last=False)

    def spread(bank, part, tile, last):
        P = R("P%d" % bank)
        grp = []
        for ii in range(4):
            i = 4 * (bank - 1) + ii
            out = T[P[0]][:, 128 * ii:128 * ii + 128]
            if part == 2:
                grp.append((out, T.SelS[:, 0:128], T[tile][:, i:V:16]))
            else:
                grp.append((out, T.AW[:, 128 * i + 1 - part:128 * i + 129 - part], A(R(tile))))
        mm(grp, [R(tile), R("SelS" if part == 2 else "AW")], [P], first=False, last=last)

    def unspread(q, bank, dst):
        for ii in range(4):
            i = 4 * (bank - 1) + ii
            oap, src, bias = T[dst][:, i:V:16], ("P%d" % bank, 128 * ii, 128 * ii + 128), col("SB", i)
            order(q, [src, bias], [])
            if q == "v":
                ins = g.vector.tensor_scalar(oap, A(src), A(bias), None, ALU.add)
            else:
                ins = g.scalar.activation(oap, A(src), ACT.Identity, bias=A(bias))
            cnt[q] += 1
            ins.then_inc(T.sem[SEM[q]], 1)
            note(q, SEM[q], cnt[q], [src, bias], [])
            log[dst] = log.get(dst, []) + [(0, V, q, SEM[q], cnt[q], True)]

    def clear_for(qs, dst):
        for q in qs:
            order(q, [], [R(dst)])
        log[dst] = []

    def send(src, dst, to, sem):
        order("g", [R(src)], [])
        rid, pid, _se = topo.addr(to)
        g.remote_dma(A(R(dst)), A(R(src)), T.sem[sem], T.sem.sent, pid, rid, topo.mask(core, to))
        sent[0] += len(topo.engines(core, to))

    def landed(b, sem, frm):
        log[b] = [(0, SCRATCH[b][1][1], "d", sem, len(topo.engines(frm, core)), True)]

    def load(q, b, out, in_, sem):
        Q[q].dma_start(out, in_).then_inc(T.sem[sem], 16)
        log[b] = [(0, SCRATCH[b][1][1], "d", sem, 16, True)]

    def quarters(out, win, lst, clamp=False, between=None):
        vgather(out, win, lst, 0, 512, clamp=clamp)
        sgather(out, win, lst, 512, 1024, clamp=clamp)
        if between:
            between()
        vgather(out, win, lst, 1024, 1536, clamp=clamp)
        sgather(out, win, lst, 1536, 2048, clamp=clamp)

    def rows_of_t(meanwhile):
        spread(1, 0, "thi", False)
        spread(3, 0, "thi", False)
        vtt(R("tlo"), R("tf"), R("thi"), ALU.subtract)
        spread(1, 1, "tlo", True)
        spread(3, 1, "tlo", True)
        for b in (2, 4):
            spread(b, 0, "thi", False)
            spread(b, 1, "tlo", True)
        for f in meanwhile:
            f()
        clear_for("vs", "S1")
        unspread("s", 1, "S1")
        unspread("v", 3, "S1")
        unspread("s", 2, "S1")
        unspread("v", 4, "S1")

    load("y", "t0i", A(R("t0i")), T.t0[:], "ldt")
    load("s", "u0i", A(R("u0i")), T.u0[:], "ldu")
    load("y", "thI", T.thI[:, 0:1], T.th[:], "ldh")
    load("y", "XB", A(R("XB")), T.x[:], "ldx")
    for r in range(RO):
        landed("fL%d" % r, "af%d" % r, nxt)
    landed("uL1", "au1", prv)
    landed("uL2", "au2", prv)
    landed("uF", "au3", prv)

    giota(col("ci", 0), [[0, 1]], 1)
    giota(R("IX"), [[1, 16], [16, 8]], 0)
    giota(R("IC"), [[1, 128]], 0)
    giota(R("M16"), [[0, 4], [16, 128]], 0)
    vset(R("AW"), 0.0)
    vcopy(col("col", 0), col("ci", 0))
    vts(col("ci", 4), col("ci", 0), 15, None, ALU.bitwise_and)
    vts(col("ci", 8), col("ci", 0), 4, None, ALU.arith_shift_right)
    vset(R("Z1"), 0.0)
    vcopy(col("col", 1), col("ci", 4))
    vcopy(col("col", 2), col("ci", 8))
    vts(R("I32"), R("IC"), col("col", 0), None, ALU.is_equal)
    vts(R("RM"), ("IC", 0, 16), col("col", 1), None, ALU.is_equal)
    fresh = log["AW"]
    for (q, w) in ((HI, 1.0), (KE - 1, 4096.0), (KE, 4096.0), (KO, 4096.0)):
        log["AW"] = fresh
        vts(R("AW"), R("IX"), col("col", 0), w, ALU.is_equal, ALU.mult, oap=T.AW[:, 1 + q:V:16])
    act(R("SelP"), R("I32"), scale=col("RM", PH))
    act(R("SB"), ("IC", 0, 16), scale=col("RM", PL))
    act(col("cw", 0), col("RM", HI), bias=col("RM", LOW))
    act(col("cw", 2), col("RM", KE), bias=col("RM", KO))
    act(col("cw", 3), col("RM", PH), bias=col("RM", KE), scale=4096.0)
    act(col("cw", 12), col("RM", PL), bias=col("RM", KE), scale=-1.0)
    act(col("cw", 7), col("cw", 2), bias=1.0)
    act(col("cw", 11), col("cw", 2), bias=4096.0, scale=-4096.5)
    act(R("d0"), ("IC", 0, 16), bias=col("cw", 7), scale=0.0)
    vcopy(R("thi"), R("t0i"))
    vcopy(R("tf"), R("t0i"))
    for b in (1, 3, 2, 4):
        prespread(b)
    giota(R("IG"), [[1, 8], [0, 16]], 0)
    blk = ("BLK", 0, 8)
    rows_of_t([lambda: vcopy(R("fS0"), R("t0i")),
               lambda: send("fS0", "fL0", prv, "af0"),
               lambda: vcopy(R("uL0"), R("u0i")),
               lambda: vts(blk, ("IC", 0, 8), col("col", 2), None, ALU.is_equal),
               lambda: vset(R("SelS"), 0.0),
               lambda: vcopy(R("Z1"), blk, oap=T.Z1[:, 15:128:16]),
               lambda: vset(R("d1"), 0.0)])
    vcopy(col("cw", 8), col("thI", 0))
    vts(R("BLF"), R("IG"), col("col", 2), None, ALU.is_equal)
    vscan(R("AB"), R("d0"), R("d1"), col("cw", 11), ALU.mult, ALU.add)
    giota(R("ZI"), [[4096, 512]], 0)
    giota(R("NEG"), [[0, V]], 0, base=-1024)

    def constants_s():
        act(R("Z01"), R("Z1"), scale=col("cw", 0))
        act(col("cw", 1), col("RM", PH), bias=col("RM", PL))
        act(col("cw", 6), col("RM", SH), bias=col("RM", SL))
        act(col("cw", 13), col("RM", KO), bias=col("RM", PL))
        act(col("cw", 5), col("RM", KE), scale=-1.0)
        act(("d0", 0, 4), ("IC", 0, 4), bias=2048.0, scale=-4096.0 * 512)
        act(col("cw", 4), col("cw", 13), bias=1.0, scale=-1.0)
        act(R("ZP"), R("Z1"), scale=col("cw", 1))
        act(col("cw", 9), col("cw", 8), bias=1.0 - 1024.0 * 6143.0, scale=2.0)
        act(col("cw", 10), col("cw", 8), bias=1024.0 * 6143.0 - 1.0, scale=-2.0)
        act(("SelS", SH - PH, 128 + SH - PH), R("I32"), scale=col("cw", 1))
        act(("RB", 0, 4), ("d0", 0, 4), bias=col("cw", 1), scale=col("cw", 2))
        act(R("ZS"), R("Z1"), scale=col("cw", 6))
        act(R("ZK"), R("Z1"), scale=col("RM", KE))
        act(R("BK"), R("BLF"), scale=col("cw", 5))
        act(R("N32"), R("I32"), scale=-1.0)
        act(R("Nb"), R("I32"), scale=-1.0)
        act(R("P0"), R("ZI"))
        act(R("MU"), R("ZI"), bias=col("cw", 4), scale=0.0)
        act(R("X2"), R("XB"), scale=2.0)

    def constants_v():
        for (z, w) in (("ZX", col("cw", 3)), ("ZO", col("RM", KO)), ("ZE", col("cw", 12))):
            vts(R(z), R("Z1"), w, None, ALU.mult)
        vts(R("ZJ"), R("Z1"), col("RM", PH), 4096.0, ALU.mult, ALU.mult)
        vts(R("BL"), R("BLF"), col("RM", PH), 4096.0, ALU.mult, ALU.mult)

    def last_constants():
        gcast(("B2", 0, 128), R("I32"))
        gcast(("B2", 128, 256), R("I32"))
        act(R("I2k"), R("I32"), scale=2048.0)
        act(R("N2"), R("I32"), scale=-2.0)
        act(R("Ix"), R("I32"), scale=2.0 ** -10)
        act(R("Ixn"), R("I32"), scale=-2.0 ** -10)
        act(R("Im64"), R("I32"), scale=-64.0)
        act(R("I4k"), R("I32"), scale=4096.0)
        act(R("N4k"), R("I32"), scale=-4096.0)
        act(("B4", 0, 128), R("I32"))
        act(("B4", 128, 256), R("I32"))

    CUT = (0, 608, 1024, 1632, 2048)
    pA, pB = ("P5", 0), ("P6", 0)
    MAGIC = 1.5 * 2.0 ** 23

    for rnd in range(RO):
        uL, fL = "uL%d" % rnd, "fL%d" % rnd
        final = rnd == RO - 1
        scatter("YB", uL, "S1", 0, V)
        if rnd == 0:
            constants_s()
            constants_v()
        for b in (1, 2, 3, 4):
            prespread(b)
        vgather("TMP", "YB", fL, 0, 1024)
        sgather("TMP", "YB", fL, 1024, V)
        vgather("YA", "TMP", uL, 0, 448)
        sgather("YA", "TMP", uL, 448, 1024)
        gcast(("CB0", 0, 448), ("YA", 0, 448))
        act(("CB0", 448, 1024), ("YA", 448, 1024))
        extract(pA, "Z01", "CB0", 0, 64)
        vgather("YA", "TMP", uL, 1024, 1600)
        gcast(("CB0", 1024, 1600), ("YA", 1024, 1600))
        act(("IN1", 0, 1024), ("YA", 0, 1024), bias=col("AB", 0))
        vgather("YA", "TMP", uL, 1600, V)
        act(("CB0", 1600, V), ("YA", 1600, V))
        extract(pB, "Z01", "CB0", 64, 128)
        act(("IN1", 1024, V), ("YA", 1024, V), bias=col("AB", 0))
        vcopy(R("uf"), R(uL))
        vcopy(("Lc", 0, 64), ("P5", 0, 64))
        cur, oth, lst = "YA", "YB", "Lc"
        for k in range(STEPS):
            more = k < STEPS - 1
            new = ("La", "Lb")[k % 2]
            for j in range(4):
                c0, c1 = CUT[j], CUT[j + 1]
                if j == 2:
                    vcopy((lst, 64, 128), ("P6", 64, 128))
                vgather(oth, cur, lst, c0, c1, in1="IN1", o=ALU.min)
                if more:
                    if j % 2 == 0:
                        gcast(("CB", c0, c1), (oth, c0, c1))
                    else:
                        act(("CB", c0, c1), (oth, c0, c1))
                        extract((pA, pB)[j // 2], "Z01", "CB", 64 * (j // 2), 64 * (j // 2) + 64)
                        act(("IN1", c1 - 1024, c1), (oth, c1 - 1024, c1), bias=col("AB", k + 1))
                elif j % 2 == 1:
                    extract((pA, pB)[j // 2], "ZK", oth, 64 * (j // 2), 64 * (j // 2) + 64)
            if more:
                vcopy((new, 0, 64), ("P5", 0, 64))
            if k == 0:
                extract(("P7", 256), "ZP", "CB0", 0, 128)
            if k == 1:
                act(R("uhi"), R("uf"))
                combine(("P7", 0, 128), [("I32", "uf"), ("Nb", "uhi")])
            if k == 2:
                act(R("ulo"), ("P7", 0, 128))
            if 3 <= k <= 6:
                spread(k - 2, 0, "uhi", False)
                spread(k - 2, 1, "ulo", False)
                spread(k - 2, 2, "CB0", True)
            if k == STEPS - 2:
                clear_for("s", "S2")
                for b in (1, 2, 3, 4):
                    unspread("s", b, "S2")
            cur, oth, lst = oth, cur, new
        Y = cur
        for b in range(4):
            mm([(A(R("P%d" % (b + 1))), A(R("BK")), A((Y, 512 * b, 512 * b + 512)))], [R("BK"), (Y, 512 * b, 512 * b + 512)], [R("P%d" % (b + 1))], last=False)

        def sub(b):
            vtt(("IN1", 512 * b, 512 * b + 512), (Y, 512 * b, 512 * b + 512), R("P0"), ALU.subtract)
            act(("TMP", 512 * b, 512 * b + 512), ("IN1", 512 * b, 512 * b + 512), ACT.Relu, bias=col("RB", b), scale=col("cw", 2))

        def scan(b):
            vscan(("WE", 512 * b, 512 * b + 512), R("MU"), ("TMP", 512 * b, 512 * b + 512), 0.0 if b == 0 else col("WE", 512 * b - 1), ALU.mult, ALU.add)

        sub(0); sub(1); sub(2); scan(0); sub(3); scan(1)
        vts(("Ll", 0, 64), ("P5", 0, 64), 2047.0, 2.0 ** -12, ALU.add, ALU.mult)
        scan(2)
        vts(("Ll", 64, 128), ("P6", 64, 128), 2047.0, 2.0 ** -12, ALU.add, ALU.mult)
        scan(3)
        act(("Kw", 0, 64), ("P5", 0, 64), bias=6144.0)
        act(("Kw", 64, 128), ("P6", 64, 128), bias=6144.0)
        vgather("LO", "WE", "Ll", 0, 1024)
        extract(pA, "ZX", "LO", 0, 64, more=[("N32", "Kw")])
        sgather("IN1", "WE", "Ll", 1536, V)
        gcast(("LO", 1536, V), ("IN1", 1536, V))
        act(R("sf"), ("P7", 256, 384))
        if rnd == 0:
            last_constants()
        vgather("LO", "WE", "Ll", 1024, 1536)
        extract(pB, "ZX", "LO", 64, 128, more=[("N32", "Kw")])
        vcopy(("Lslot", 0, 64), ("P5", 0, 64))
        act(("slotf", 0, 64), ("P5", 0, 64))
        scatter("RW", "Lslot", "S2", 0, 512)
        extract(("P7", 0), "ZO", "LO", 0, 128)
        vcopy(("Lslot", 64, 128), ("P6", 64, 128))
        scatter("RW", "Lslot", "S2", 512, V)

        def limit(b):
            c0, c1, P = 512 * b, 512 * b + 512, R("P%d" % (b + 1))
            mm([(A(P), A(R("BL")), A(("LO", c0, c1))), (A(P), A(R("Ix")), A(("X2", c0, c1)))],
               [R("BL"), R("Ix"), ("LO", c0, c1), ("X2", c0, c1)], [P], first=False, last=b > 0)

        def limit_s(b):
            act(("IN2", 512 * b, 512 * b + 512), R("P%d" % (b + 1)), bias=col("cw", 9), scale=1024.0)

        g1, g2, g3 = ("P5", 128, 256), ("P7", 384, 512), ("P6", 128, 256)
        act(R("a1"), ("P7", 0, 128), bias=MAGIC, scale=0.5 - 2.0 ** -13)
        act(R("of"), ("P7", 0, 128))
        act(R("af"), R("a1"), bias=-MAGIC)
        act(("slotf", 64, 128), ("P6", 64, 128))
        extract(("P5", 128), "ZJ", "LO", 0, 128, more=[("N32", "Kw")], last=False)
        combine(g1, [("I32", "af")], first=False)
        act(R("sg"), g1, ACT.Sign, bias=0.5)
        combine(g3, [("I32", "slotf"), ("I32", "af")], last=False)
        combine(g2, [("I32", "of"), ("I2k", "sg")])
        act(R("mo"), g2, ACT.Relu, bias=-2048.0)
        limit(1)
        combine(g3, [("N32", "mo")], first=False)
        limit_s(1)
        vcopy(R("Lsh"), g3)
        limit(2)
        limit(3)
        limit_s(2)
        extract(("P7", 128), "ZE", "LO", 0, 128)
        limit_s(3)
        limit(0)
        extract(("P7", 0), "ZP", "RW", 0, 128)
        vgather("HB", "RW", "Lsh", 0, 512)
        sgather("HB", "RW", "Lsh", 512, 1024)
        extract(pA, "ZP", "HB", 0, 64)
        vgather("HB", "RW", "Lsh", 1024, 1408)
        sgather("HB", "RW", "Lsh", 1408, V)
        extract(pB, "ZP", "HB", 64, 128)
        vcopy(R("LL"), ("P7", 0, 384))
        vcopy(("Lhalf", 0, 64), ("P5", 0, 64))
        vgather("TMP", "X2", "Lhalf", 512, 1024, in1="IN2", o=ALU.subtract)
        op("s", lambda: g.scalar.activation(A(R("XA")), ind("X2", "Lhalf", 0, 512), ACT.Identity), [R("X2"), ("Lhalf", 0, 32)], [R("XA")])
        vcopy(("Lhalf", 64, 128), ("P6", 64, 128))
        combine(R("P1"), [("Ixn", "XA")], first=False)
        act(("TMP", 0, 512), R("P1"), bias=col("cw", 10), scale=-1024.0)
        vgather("TMP", "X2", "Lhalf", 1024, V, in1="IN2", o=ALU.subtract)
        combine(("P5", 256, 384), [("I32", "of"), ("N2", "af")])
        act(R("odd"), ("P5", 256, 384))
        extract(("P7", 128), "Z01", "HB", 0, 128, more=[("N32", "uf")])
        combine(("P5", 128, 256), [("I32", "tf"), ("I4k", "odd")])
        combine(("P5", 256, 384), [("I32", "sf"), ("N4k", "odd")])
        extract(("P7", 256), "ZS", "HB", 0, 128, more=[("N32", "sf")])
        vgather("IN1", "TMP", "LR", 0, 640)
        for (c0, c1) in ((640, 1152), (1152, 1600), (1600, V)):
            sgather("IN1", "TMP", "LR", c0, c1)
        act(R("r1"), ("P5", 128, 256), ACT.Relu, bias=-4096.0)
        act(R("r2"), ("P5", 256, 384), ACT.Relu)
        combine(("P7", 384, 512), [("I32", "r1"), ("I32", "r2")])
        if not final:
            for b in (1, 3, 2, 4):
                prespread(b)
        for (c0, c1) in ((0, 1152), (1152, 1600), (1600, V)):
            vscan(("ST", c0, c1), ("NEG", c0, c1), ("IN1", c0, c1), col("ST", c0 - 1) if c0 else -4096.0, ALU.add, ALU.max)
        quarters("EG", "ST", "Lend", clamp=True, between=lambda: extract(pA, "Z1", "EG", 0, 64, more=[("Im64", "odd")]))
        extract(pA, "Z1", "EG", 64, 128, more=[("Im64", "odd")])
        hP = ("P5", 128, 256)
        c0, c1 = 128 - 16 * GS, 256 - 16 * GS
        vgather("EGS", "EG", "Ls", 0, 320)
        sgather("EGS", "EG", "Ls", 320, 1024)
        vts(R("Tn"), ("P5", 0, 128), -1.0, None, ALU.is_lt)
        mm([(A(hP), A(("B4", c0, c1)), A(R("uf")))], [R("B4"), R("uf")], [hP], last=False)
        vtt(R("pu"), ("P7", 128, 256), R("Tn"), ALU.mult)
        mm([(A(hP), A(("B2", c0, c1)), A(R("pu")))], [R("B2"), R("pu")], [hP], first=False)
        extract(pB, "Z1", "EGS", 0, 64, more=[("Im64", "odd")])
        hs = "hF" if final else "hS%d" % rnd
        vcopy(R(hs), hP)
        send(hs, "uF" if final else "uL%d" % (rnd + 1), nxt, "au%d" % (rnd + 1))
        vgather("EGS", "EG", "Ls", 1024, 1408)
        sgather("EGS", "EG", "Ls", 1408, V)
        extract(pB, "Z1", "EGS", 64, 128, more=[("Im64", "odd")])
        vts(R("Ts"), ("P6", 0, 128), -1.0, None, ALU.is_lt)
        vtt(R("xr"), R("Ts"), R("Tn"), ALU.not_equal)
        vtt(R("p2"), ("P7", 256, 384), R("xr"), ALU.mult)
        if not final:
            vtt(R("thi"), ("P7", 384, 512), R("p2"), ALU.add)
        vtt(R("tf"), ("P7", 384, 512), R("p2"), ALU.add)
        if not final:
            rows_of_t([lambda: vcopy(R("fS%d" % (rnd + 1)), R("tf")),
                       lambda: send("fS%d" % (rnd + 1), "fL%d" % (rnd + 1), prv, "af%d" % (rnd + 1))])

    order("y", [R("tf")], [])
    g.sync.dma_start(T.yt[:], A(R("tf"))).then_inc(T.sem.out, 16)
    order("s", [R("uF")], [])
    g.scalar.dma_start(T.yu[:], A(R("uF"))).then_inc(T.sem.out, 16)
    for q in ("v", "s", "p", "g"):
        wait("g", SEM[q], cnt[q])
    wait("g", "sent", sent[0])
    wait("g", "out", 32)
